import numpy as np
import ml_dtypes


def mxq(x, axis, fmt="e4m3"):
    dtype, down = {"e4m3": (ml_dtypes.float8_e4m3fn, 7), "e5m2": (ml_dtypes.float8_e5m2, 14)}[fmt]
    v = np.moveaxis(np.asarray(x, np.float32).astype(ml_dtypes.bfloat16).astype(np.float64), axis, -1)
    blocks = v.reshape(v.shape[:-1] + (-1, 32))
    amax = np.abs(blocks).max(-1, keepdims=True)
    byte = np.maximum(np.where(amax > 0, np.frexp(amax)[1] - 1 + 127, 0) - down, 1)
    scale = np.exp2(byte - 127.0)
    codes = (blocks / scale).astype(np.float32).astype(dtype).astype(np.float64)
    return np.moveaxis((codes * scale).reshape(v.shape), -1, axis)


WIDE = False


def mx_kscale(k):
    if not WIDE:
        return np.ones(k)
    levels = np.array([30, -30])
    if k % 512:
        return np.exp2(np.random.permutation(np.resize(levels, k // 32))).repeat(32)
    a = np.empty((k // 512, 16))
    for p in range(k // 512):
        a[p, :8] = np.random.permutation(np.resize(levels, 8))
        for g in range(8):
            far = levels[np.abs(levels - a[p, g]) >= 10]
            a[p, g + 8] = far[np.random.randint(len(far))]
    return np.exp2(a.ravel()).repeat(32)


def f64(x):
    return np.asarray(x).astype(np.float64)


def striped(idx):
    return np.tile(np.asarray(idx).reshape(-1, 16).T, (8, 1)).astype(np.uint16)


def unstriped(offs):
    return offs[:16].T.reshape(-1).astype(np.int64)


E2M1 = np.array([0.0, 0.5, 1.0, 1.5, 2.0, 3.0, 4.0, 6.0, -0.0, -0.5, -1.0, -1.5, -2.0, -3.0, -4.0, -6.0])


def pack_weight(w, fmt):
    k, n = w.shape
    w = f64(np.asarray(w, np.float32).astype(ml_dtypes.bfloat16)).reshape(k // 32, 32, n)
    amax = np.abs(w).max(1)
    if fmt in ("e4m3", "e5m2"):
        byte = np.frexp(amax)[1] - 1 + 127 - (7 if fmt == "e4m3" else 14)
    else:
        mant, ex = np.frexp(amax / 6.0)
        byte = np.where(mant > 0.5, ex, ex - 1) + 127
    byte = np.clip(np.where(amax > 0, byte, 1), 1, 254)
    scaled = (w * np.exp2(127.0 - byte)[:, None, :]).reshape(k, n).astype(np.float32)
    by_word = np.ascontiguousarray(scaled.reshape(k // 512, 128, 4, n).transpose(0, 1, 3, 2))
    if fmt in ("e4m3", "e5m2"):
        words = by_word.astype(ml_dtypes.float8_e4m3fn if fmt == "e4m3" else ml_dtypes.float8_e5m2).view(np.uint8)
    else:
        c = by_word.astype(ml_dtypes.float4_e2m1fn).view(np.uint8) & 0xF
        words = (c[..., 0::2] | (c[..., 1::2] << 4)).reshape(k // 512, 128, 2 * n)
    return np.ascontiguousarray(words), np.ascontiguousarray(byte.astype(np.uint8).reshape(k // 512, 16, n))


def unpack_weight(words, scales, fmt):
    g, _, n = scales.shape
    words = np.ascontiguousarray(words).reshape(g, 128, n, -1)
    if fmt in ("e4m3", "e5m2"):
        vals = words.view(ml_dtypes.float8_e4m3fn if fmt == "e4m3" else ml_dtypes.float8_e5m2).astype(np.float64)
    else:
        nib = np.empty((g, 128, n, 4), np.uint8)
        nib[..., 0::2] = words & 0xF
        nib[..., 1::2] = words >> 4
        vals = E2M1[nib]
    vals = vals * np.repeat(np.exp2(scales.astype(np.float64) - 127.0), 8, axis=1)[..., None]
    return vals.transpose(0, 1, 3, 2).reshape(g * 512, n)


K, T, J, R, F, Z, G, N = 512, 512, 256, 512, 512, 1024, 32, 256


def setup_inputs():
    n = np.random.standard_normal
    idx = np.random.permutation(T)[:J]
    idx2 = np.random.permutation(T)[:J]
    idx3 = np.random.permutation(Z)[:J]
    fk = mx_kscale(K)
    fr = mx_kscale(R)
    ff = mx_kscale(F)
    wp = pack_weight(n((K, R)) * 1 / np.sqrt(K) * fk[:, None] * fr, "e2m1")
    xop = pack_weight(n((F, Z)) / ff[:, None], "e4m3")
    w2p = pack_weight(n((F, R)) * 1 / np.sqrt(F) * ff[:, None] * fr, "e5m2")
    wbp = pack_weight(n((R, N)) * 1 / np.sqrt(R) / fr[:, None], "e5m2")
    return {
        "xf": (n((K, T))).astype(np.float32),
        "fk": (np.random.uniform(0.5, 2.0, (K, 1)) / fk[:, None]).astype(np.float32),
        "w_words": wp[0],
        "w_scales": wp[1],
        "xo_words": xop[0],
        "xo_scales": xop[1],
        "w2_words": w2p[0],
        "w2_scales": w2p[1],
        "wb_words": wbp[0],
        "wb_scales": wbp[1],
        "bi": (np.random.uniform(-0.5, 0.5, (1, N))).astype(np.float32),
        "offs": striped(idx),
        "offs2": striped(idx2),
        "offs3": striped(idx3),
    }


def reference(xf, fk, w_words, w_scales, xo_words, xo_scales, w2_words, w2_scales, wb_words, wb_scales, bi, offs, offs2, offs3):
    idx = unstriped(offs)
    idx2 = unstriped(offs2)
    idx3 = unstriped(offs3)
    wu = unpack_weight(w_words, w_scales, "e2m1")
    xou = unpack_weight(xo_words, xo_scales, "e4m3")
    w2u = unpack_weight(w2_words, w2_scales, "e5m2")
    wbu = unpack_weight(wb_words, wb_scales, "e5m2")
    u = np.maximum(f64(xf)[:, idx], f64(xf)[:, idx2]) * f64(fk)
    uq = mxq(u, 0, "e4m3")
    xoidx3g = xou[:, idx3]
    a = wu.T @ uq + w2u.T @ xoidx3g
    m1 = a.reshape(R, G, J // G).mean(axis=2)
    m2 = np.repeat(m1, J // G, axis=1)
    hid = a - m2
    hidq = mxq(hid, 0, "e5m2")
    p = hidq.T @ wbu
    ea = np.exp(0.7 * p + f64(bi))
    y = 256.0 * ea / np.sum(ea, axis=1, keepdims=True)
    return y

@@ -1,0 +1,214 @@
+from contextlib import ExitStack
+
+import concourse.mybir as mybir
+
+K, T, J, R, F, Z, N = 512, 512, 256, 512, 512, 1024, 256
+FLOPS = 2 * K * R * J + 2 * F * R * J + 2 * R * J * N
+
+F32 = mybir.dt.float32
+BF16 = mybir.dt.bfloat16
+I32 = mybir.dt.int32
+U32 = mybir.dt.uint32
+U16 = mybir.dt.uint16
+U8 = mybir.dt.uint8
+E4M3 = mybir.dt.float8_e4m3fn_x4
+E5M2 = mybir.dt.float8_e5m2_x4
+E2M1 = mybir.dt.float4_e2m1fn_x4
+ALU = mybir.AluOpType
+ACT = mybir.ActivationFunctionType
+AX = mybir.AxisListType
+
+P = 128
+PACK = 4
+HALF = 128
+BUNDLE = 8
+
+
+def load_scale_rows(queue, plane, scales, quadrants):
+    for q in quadrants:
+        queue.dma_start(out=plane[32 * q : 32 * q + 4, :].bitcast(I32), in_=scales[0, 4 * q : 4 * q + 4, :].bitcast(I32))
+
+
+def tile_list_sum_largerpicks_othertable_levelled_rowshares_kernel(
+    tc, xf, fk, w_words, w_scales, xo_words, xo_scales, w2_words, w2_scales, wb_words, wb_scales, bi, offs, offs2, offs3, out
+):
+    nc = tc.nc
+    with ExitStack() as ctx:
+        sb = ctx.enter_context(tc.tile_pool(name="sb", bufs=1))
+        ps = ctx.enter_context(tc.psum_pool(name="ps", bufs=1))
+
+        list1 = sb.tile([P, J // 16], U16, name="list1")
+        list2 = sb.tile([P, J // 16], U16, name="list2")
+        list3 = sb.tile([P, J // 16], U16, name="list3")
+        x0 = sb.tile([P, T], F32, name="x0")
+        x1 = sb.tile([P, T], F32, name="x1")
+        x23 = sb.tile([P, 2, T], F32, name="x23")
+        x_planes = (x0[:], x1[:], x23[:, 0, :], x23[:, 1, :])
+        fk_sb = sb.tile([P, PACK], F32, name="fk_sb")
+        w_raw = sb.tile([P, R], U16, name="w_raw")
+        w2_raw = sb.tile([P, R], U32, name="w2_raw")
+        ws_raw = sb.tile([P, R], U8, name="ws_raw", tag="ws_raw", align_bytes=64)
+        w2s_raw = sb.tile([P, R], U8, name="w2s_raw")
+        xo_tab = sb.tile([P, Z], U32, name="xo_tab", tag="xo_tab")
+        xos_tab = sb.tile([P, Z], U8, name="xos_tab", tag="xos_tab", align_bytes=64)
+        wb_sb = sb.tile([P, N], U32, name="wb_sb", align_bytes=64)
+        wbs_sb = sb.tile([P, N], U8, name="wbs_sb", align_bytes=64)
+        bi_sb = sb.tile([P, N], F32, name="bi_sb")
+
+        nc.gpsimd.memset(w2s_raw[:].bitcast(I32), 0)
+        for plane in (xos_tab, ws_raw, wbs_sb):
+            nc.vector.memset(plane[:].bitcast(I32), 0)
+
+        xv = xf.rearrange("(p t) c -> p t c", t=PACK)
+        nc.sync.dma_start(out=x0[:], in_=xv[:, 0, :])
+        nc.sync.dma_start(list1[:], offs)
+        nc.sync.dma_start(list2[:], offs2)
+        load_scale_rows(nc.scalar, w2s_raw, w2_scales, range(3))
+        warm = sb.tile([P, 1], F32, name="warm")
+        nc.vector.memset(warm[:], 0.0)
+        nc.scalar.activation(warm[:], warm[:], ACT.Exp)
+        nc.sync.dma_start(out=x1[:], in_=xv[:, 1, :])
+        nc.sync.dma_start(out=x23[:], in_=xv[:, 2:4, :])
+        nc.gpsimd.dma_start(out=fk_sb[:], in_=fk.rearrange("(p t) o -> p (t o)", t=PACK))
+        load_scale_rows(nc.gpsimd, ws_raw, w_scales, range(3, 4))
+        nc.sync.dma_start(out=xo_tab[:].bitcast(I32), in_=xo_words[0].rearrange("p n t -> p (n t)").bitcast(I32))
+        nc.sync.dma_start(list3[:], offs3)
+        load_scale_rows(nc.sync, w2s_raw, w2_scales, range(3, 4))
+        load_scale_rows(nc.sync, xos_tab, xo_scales, range(3))
+        nc.sync.dma_start(out=w2_raw[:].bitcast(I32), in_=w2_words[0].rearrange("p n t -> p (n t)").bitcast(I32))
+        load_scale_rows(nc.sync, xos_tab, xo_scales, range(3, 4))
+        nc.sync.dma_start(out=w_raw[:].bitcast(I32), in_=w_words[0].bitcast(I32))
+        load_scale_rows(nc.sync, ws_raw, w_scales, range(3))
+        nc.sync.dma_start(out=wb_sb[:].bitcast(I32), in_=wb_words[0].rearrange("p n t -> p (n t)").bitcast(I32))
+        load_scale_rows(nc.sync, wbs_sb, wb_scales, range(4))
+        nc.sync.dma_start(out=bi_sb[:], in_=bi[0].partition_broadcast(P))
+
+        w_st = sb.tile([P, R], U16, name="w_st", align_bytes=64)
+        w2_st = sb.tile([P, R], U32, name="w2_st", align_bytes=64)
+        ws_st = sb.tile([P, R], U8, name="ws_st", align_bytes=64)
+        w2s_st = sb.tile([P, R], U8, name="w2s_st", align_bytes=64)
+
+        def deal(copy, dst, raw):
+            copy(dst[:].rearrange("p (t q) -> p t q", t=PACK), raw[:].rearrange("p (q t) -> p t q", t=PACK))
+
+        pick1 = sb.tile([P, PACK, J], F32, name="pick1")
+        xo_g = sb.tile([P, J], U32, name="xo_g", align_bytes=64)
+        xos_g = sb.tile([P, J], U8, name="xos_g", align_bytes=64)
+        pick2 = []
+        for t in range(PACK):
+            nc.scalar.activation(pick1[:, t, :], x_planes[t].indirect(list1[:]), ACT.Copy)
+            if t == PACK - 1:
+                nc.vector.tensor_copy(xo_g[:], xo_tab[:].indirect(list3[:]))
+            picked = sb.tile([P, J], F32, name=f"pick2_{t}", tag="xo_tab" if t == PACK - 1 else f"pick2_{t}")
+            if t < 2:
+                nc.vector.tensor_copy(picked[:], x_planes[t].indirect(list2[:]))
+            else:
+                nc.scalar.activation(picked[:], x_planes[t].indirect(list2[:]), ACT.Copy)
+            pick2.append(picked)
+        deal(nc.vector.tensor_copy, w2s_st, w2s_raw)
+        nc.vector.tensor_copy(xos_g[:], xos_tab[:].indirect(list3[:]))
+        larger = sb.tile([P, PACK, J], F32, name="larger")
+        for t in range(PACK):
+            nc.vector.tensor_tensor(larger[:, t, :], pick1[:, t, :], pick2[t][:], ALU.max)
+
+        deal(nc.scalar.copy, w2_st, w2_raw)
+        deal(nc.scalar.copy, w_st, w_raw)
+        deal(nc.vector.tensor_copy, ws_st, ws_raw)
+
+        halves = range(J // HALF)
+        acc = [ps.tile([P, PACK, HALF], F32, name=f"acc{h}") for h in halves]
+        for h in halves:
+            cols = slice(h * HALF, (h + 1) * HALF)
+            for t in range(PACK):
+                st = slice(t * P, (t + 1) * P)
+                nc.tensor.matmul_mx(
+                    out=acc[h][:, t, :],
+                    lhsT=w2_st[:, st].bitcast(E5M2),
+                    lhsT_scale=w2s_st[:, st],
+                    rhs=xo_g[:, cols].bitcast(E4M3),
+                    rhs_scale=xos_g[:, cols],
+                    start=(t == 0),
+                    stop=False,
+                )
+
+        for h in halves:
+            cols = slice(h * HALF, (h + 1) * HALF)
+            u_bf = sb.tile([P, HALF, PACK], BF16, name=f"u_bf{h}", tag=("xos_tab", "ws_raw")[h], align_bytes=64)
+            nc.vector.tensor_tensor(
+                u_bf[:],
+                larger[:, :, cols].rearrange("p t j -> p j t"),
+                fk_sb[:].unsqueeze(1).to_broadcast([P, HALF, PACK]),
+                ALU.mult,
+            )
+            uq = sb.tile([P, HALF], U32, name=f"uq{h}", align_bytes=64)
+            us = sb.tile([P, HALF], U8, name=f"us{h}", align_bytes=64)
+            nc.vector.quantize_mx(out=uq[:].bitcast(E4M3), scales=us[:], in_=u_bf[:].rearrange("p j t -> p (j t)"))
+            for t in range(PACK):
+                st = slice(t * P, (t + 1) * P)
+                nc.tensor.matmul_mx(
+                    out=acc[h][:, t, :],
+                    lhsT=w_st[:, st].bitcast(E2M1),
+                    lhsT_scale=ws_st[:, st],
+                    rhs=uq[:].bitcast(E4M3),
+                    rhs_scale=us[:],
+                    start=False,
+                    stop=(t == PACK - 1),
+                )
+
+        G = HALF // BUNDLE
+        means = []
+        for h in halves:
+            sums = sb.tile([P, G, PACK], F32, name=f"sums{h}", tag=("ws_raw", "sums1")[h], align_bytes=64)
+            nc.vector.tensor_reduce(
+                out=sums[:], in_=acc[h][:].rearrange("p t (g e) -> p g t e", e=BUNDLE), axis=AX.X, op=ALU.add
+            )
+            mean = sb.tile([P, G, PACK], F32, name=f"mean{h}")
+            nc.scalar.activation(mean[:], sums[:], ACT.Copy, scale=1.0 / BUNDLE)
+            means.append(mean)
+
+        hids = []
+        for h in halves:
+            hid = sb.tile([P, G, BUNDLE, PACK], BF16, name=f"hid{h}", align_bytes=64)
+            nc.vector.tensor_tensor(
+                hid[:],
+                acc[h][:].rearrange("p t (g e) -> p g e t", e=BUNDLE),
+                means[h][:].unsqueeze(2).to_broadcast([P, G, BUNDLE, PACK]),
+                ALU.subtract,
+            )
+            hids.append(hid)
+
+        logits = []
+        for h in halves:
+            hq = sb.tile([P, HALF], U32, name=f"hq{h}", align_bytes=64)
+            hs = sb.tile([P, HALF], U8, name=f"hs{h}", align_bytes=64)
+            nc.vector.quantize_mx(out=hq[:].bitcast(E5M2), scales=hs[:], in_=hids[h][:].rearrange("p g e t -> p (g e t)"))
+            prod = ps.tile([P, N], F32, name=f"prod{h}")
+            nc.tensor.matmul_mx(
+                out=prod[:],
+                lhsT=hq[:].bitcast(E5M2),
+                lhsT_scale=hs[:],
+                rhs=wb_sb[:].bitcast(E5M2),
+                rhs_scale=wbs_sb[:],
+                start=True,
+                stop=True,
+            )
+            logits.append(prod)
+
+        exps = []
+        for h in halves:
+            z = sb.tile([P, N], F32, name=f"z{h}")
+            nc.vector.scalar_tensor_tensor(z[:], logits[h][:], 0.7, bi_sb[:], ALU.mult, ALU.add)
+            neg_max = sb.tile([P, 1], F32, name=f"neg_max{h}")
+            nc.vector.tensor_reduce(out=neg_max[:], in_=z[:], axis=AX.X, op=ALU.max, negate=True)
+            e = sb.tile([P, N], F32, name=f"e{h}")
+            total = sb.tile([P, 1], F32, name=f"total{h}")
+            nc.scalar.activation(e[:], z[:], ACT.Exp, bias=neg_max[:], scale=1.0, accum_out=total[:])
+            exps.append((e, total))
+
+        for h in halves:
+            e, total = exps[h]
+            inv = sb.tile([P, 1], F32, name=f"inv{h}")
+            nc.vector.reciprocal(inv[:], total[:])
+            y = sb.tile([P, N], F32, name=f"y{h}")
+            nc.vector.tensor_scalar(y[:], e[:], inv[:], 256.0, ALU.mult, ALU.mult)
+            nc.sync.dma_start(out=out[h * HALF : (h + 1) * HALF, :], in_=y[:])

@@ -64,9 +64,6 @@ def tile_list_sum_largerpicks_othertable_levelled_rowshares_kernel(
         nc.sync.dma_start(list1[:], offs)
         nc.sync.dma_start(list2[:], offs2)
         load_scale_rows(nc.scalar, w2s_raw, w2_scales, range(3))
-        warm = sb.tile([P, 1], F32, name="warm")
-        nc.vector.memset(warm[:], 0.0)
-        nc.scalar.activation(warm[:], warm[:], ACT.Exp)
         nc.sync.dma_start(out=x1[:], in_=xv[:, 1, :])
         nc.sync.dma_start(out=x23[:], in_=xv[:, 2:4, :])
         nc.gpsimd.dma_start(out=fk_sb[:], in_=fk.rearrange("(p t) o -> p (t o)", t=PACK))

@@ -40,17 +40,15 @@ def tile_list_sum_largerpicks_othertable_levelled_rowshares_kernel(
         list1 = sb.tile([P, J // 16], U16, name="list1")
         list2 = sb.tile([P, J // 16], U16, name="list2")
         list3 = sb.tile([P, J // 16], U16, name="list3")
-        x0 = sb.tile([P, T], F32, name="x0")
-        x1 = sb.tile([P, T], F32, name="x1")
-        x23 = sb.tile([P, 2, T], F32, name="x23")
-        x_planes = (x0[:], x1[:], x23[:, 0, :], x23[:, 1, :])
+        x_pairs = [sb.tile([P, 2, T], F32, name=f"x{u}") for u in range(2)]
+        x_planes = [x_pairs[t // 2][:, t % 2, :] for t in range(PACK)]
         fk_sb = sb.tile([P, PACK], F32, name="fk_sb")
         w_raw = sb.tile([P, R], U16, name="w_raw")
         w2_raw = sb.tile([P, R], U32, name="w2_raw")
         ws_raw = sb.tile([P, R], U8, name="ws_raw", tag="ws_raw", align_bytes=64)
         w2s_raw = sb.tile([P, R], U8, name="w2s_raw")
-        xo_tab = sb.tile([P, Z], U32, name="xo_tab", tag="xo_tab")
-        xos_tab = sb.tile([P, Z], U8, name="xos_tab", tag="xos_tab", align_bytes=64)
+        xo_tab = sb.tile([P, Z], U32, name="xo_tab", tag="xo_tab", align_bytes=64)
+        xos_tab = sb.tile([P, Z], U8, name="xos_tab")
         wb_sb = sb.tile([P, N], U32, name="wb_sb", align_bytes=64)
         wbs_sb = sb.tile([P, N], U8, name="wbs_sb", align_bytes=64)
         bi_sb = sb.tile([P, N], F32, name="bi_sb")
@@ -60,57 +58,65 @@ def tile_list_sum_largerpicks_othertable_levelled_rowshares_kernel(
             nc.vector.memset(plane[:].bitcast(I32), 0)
 
         xv = xf.rearrange("(p t) c -> p t c", t=PACK)
-        nc.sync.dma_start(out=x0[:], in_=xv[:, 0, :])
         nc.sync.dma_start(list1[:], offs)
         nc.sync.dma_start(list2[:], offs2)
+        nc.sync.dma_start(list3[:], offs3)
         load_scale_rows(nc.scalar, w2s_raw, w2_scales, range(3))
-        nc.sync.dma_start(out=x1[:], in_=xv[:, 1, :])
-        nc.sync.dma_start(out=x23[:], in_=xv[:, 2:4, :])
+        warm = sb.tile([P, 1], F32, name="warm")
+        nc.vector.memset(warm[:], 0.0)
+        nc.scalar.activation(warm[:], warm[:], ACT.Exp)
+        nc.sync.dma_start(out=x_pairs[0][:], in_=xv[:, 0:2, :])
+        nc.sync.dma_start(out=x_pairs[1][:], in_=xv[:, 2:4, :])
         nc.gpsimd.dma_start(out=fk_sb[:], in_=fk.rearrange("(p t) o -> p (t o)", t=PACK))
         load_scale_rows(nc.gpsimd, ws_raw, w_scales, range(3, 4))
-        nc.sync.dma_start(out=xo_tab[:].bitcast(I32), in_=xo_words[0].rearrange("p n t -> p (n t)").bitcast(I32))
-        nc.sync.dma_start(list3[:], offs3)
         load_scale_rows(nc.sync, w2s_raw, w2_scales, range(3, 4))
-        load_scale_rows(nc.sync, xos_tab, xo_scales, range(3))
+        load_scale_rows(nc.sync, xos_tab, xo_scales, range(1))
+        nc.sync.dma_start(out=xo_tab[:].bitcast(I32), in_=xo_words[0].rearrange("p n t -> p (n t)").bitcast(I32))
         nc.sync.dma_start(out=w2_raw[:].bitcast(I32), in_=w2_words[0].rearrange("p n t -> p (n t)").bitcast(I32))
-        load_scale_rows(nc.sync, xos_tab, xo_scales, range(3, 4))
         nc.sync.dma_start(out=w_raw[:].bitcast(I32), in_=w_words[0].bitcast(I32))
+        load_scale_rows(nc.sync, xos_tab, xo_scales, range(1, 4))
         load_scale_rows(nc.sync, ws_raw, w_scales, range(3))
         nc.sync.dma_start(out=wb_sb[:].bitcast(I32), in_=wb_words[0].rearrange("p n t -> p (n t)").bitcast(I32))
         load_scale_rows(nc.sync, wbs_sb, wb_scales, range(4))
         nc.sync.dma_start(out=bi_sb[:], in_=bi[0].partition_broadcast(P))
 
-        w_st = sb.tile([P, R], U16, name="w_st", align_bytes=64)
         w2_st = sb.tile([P, R], U32, name="w2_st", align_bytes=64)
         ws_st = sb.tile([P, R], U8, name="ws_st", align_bytes=64)
         w2s_st = sb.tile([P, R], U8, name="w2s_st", align_bytes=64)
 
-        def deal(copy, dst, raw):
-            copy(dst[:].rearrange("p (t q) -> p t q", t=PACK), raw[:].rearrange("p (q t) -> p t q", t=PACK))
+        def deal(copy, dst, raw, order):
+            copy(dst[:].rearrange("p (t q) -> " + order, t=PACK), raw[:].rearrange("p (q t) -> " + order, t=PACK))
 
+        deal(nc.vector.tensor_copy, w2s_st, w2s_raw, "p t q")
         pick1 = sb.tile([P, PACK, J], F32, name="pick1")
+        pick2 = sb.tile([P, PACK, J], F32, name="pick2")
         xo_g = sb.tile([P, J], U32, name="xo_g", align_bytes=64)
         xos_g = sb.tile([P, J], U8, name="xos_g", align_bytes=64)
-        pick2 = []
         for t in range(PACK):
             nc.scalar.activation(pick1[:, t, :], x_planes[t].indirect(list1[:]), ACT.Copy)
-            if t == PACK - 1:
-                nc.vector.tensor_copy(xo_g[:], xo_tab[:].indirect(list3[:]))
-            picked = sb.tile([P, J], F32, name=f"pick2_{t}", tag="xo_tab" if t == PACK - 1 else f"pick2_{t}")
-            if t < 2:
-                nc.vector.tensor_copy(picked[:], x_planes[t].indirect(list2[:]))
+            if t in (2,):
+                nc.scalar.activation(pick2[:, t, :], x_planes[t].indirect(list2[:]), ACT.Copy)
             else:
-                nc.scalar.activation(picked[:], x_planes[t].indirect(list2[:]), ACT.Copy)
-            pick2.append(picked)
-        deal(nc.vector.tensor_copy, w2s_st, w2s_raw)
+                nc.vector.tensor_copy(pick2[:, t, :], x_planes[t].indirect(list2[:]))
+        larger01 = sb.tile([P, 2, J], F32, name="larger01")
+        nc.vector.tensor_tensor(larger01[:], pick1[:, 0:2, :], pick2[:, 0:2, :], ALU.max)
+        nc.vector.tensor_copy(xo_g[:], xo_tab[:].indirect(list3[:]))
+        larger23 = sb.tile([P, 2, J], F32, name="larger23", tag="xo_tab", align_bytes=64)
+        nc.vector.tensor_tensor(larger23[:], pick1[:, 2:4, :], pick2[:, 2:4, :], ALU.max)
         nc.vector.tensor_copy(xos_g[:], xos_tab[:].indirect(list3[:]))
-        larger = sb.tile([P, PACK, J], F32, name="larger")
-        for t in range(PACK):
-            nc.vector.tensor_tensor(larger[:, t, :], pick1[:, t, :], pick2[t][:], ALU.max)
-
-        deal(nc.scalar.copy, w2_st, w2_raw)
-        deal(nc.scalar.copy, w_st, w_raw)
-        deal(nc.vector.tensor_copy, ws_st, ws_raw)
+        deal(nc.scalar.copy, w2_st, w2_raw, "p q t")
+        u_planes = sb.tile([P, PACK, J], BF16, name="u_planes")
+        for t in range(2):
+            nc.scalar.activation(u_planes[:, t, :], larger01[:, t, :], ACT.Copy, scale=fk_sb[:, t : t + 1])
+        for j0 in range(0, J, HALF):
+            for t in range(2, PACK):
+                nc.scalar.activation(
+                    u_planes[:, t, j0 : j0 + HALF], larger23[:, t - 2, j0 : j0 + HALF], ACT.Copy, scale=fk_sb[:, t : t + 1]
+                )
+        w_st = sb.tile([P, R], U16, name="w_st", tag="xo_tab", align_bytes=64)
+        deal(nc.scalar.copy, w_st, w_raw, "p q t")
+        deal(nc.vector.tensor_copy, ws_st, ws_raw, "p t q")
+        u_all = sb.tile([P, J, PACK], BF16, name="u_all", tag="ws_raw", align_bytes=64)
 
         halves = range(J // HALF)
         acc = [ps.tile([P, PACK, HALF], F32, name=f"acc{h}") for h in halves]
@@ -130,16 +136,14 @@ def tile_list_sum_largerpicks_othertable_levelled_rowshares_kernel(
 
         for h in halves:
             cols = slice(h * HALF, (h + 1) * HALF)
-            u_bf = sb.tile([P, HALF, PACK], BF16, name=f"u_bf{h}", tag=("xos_tab", "ws_raw")[h], align_bytes=64)
-            nc.vector.tensor_tensor(
-                u_bf[:],
-                larger[:, :, cols].rearrange("p t j -> p j t"),
-                fk_sb[:].unsqueeze(1).to_broadcast([P, HALF, PACK]),
-                ALU.mult,
+            u_bf = u_all[:, cols, :]
+            nc.vector.tensor_copy(
+                u_bf.rearrange("p (c i) t -> p c t i", i=4),
+                u_planes[:, :, cols].rearrange("p t (c i) -> p c t i", i=4),
             )
             uq = sb.tile([P, HALF], U32, name=f"uq{h}", align_bytes=64)
             us = sb.tile([P, HALF], U8, name=f"us{h}", align_bytes=64)
-            nc.vector.quantize_mx(out=uq[:].bitcast(E4M3), scales=us[:], in_=u_bf[:].rearrange("p j t -> p (j t)"))
+            nc.vector.quantize_mx(out=uq[:].bitcast(E4M3), scales=us[:], in_=u_bf.rearrange("p j t -> p (j t)"))
             for t in range(PACK):
                 st = slice(t * P, (t + 1) * P)
                 nc.tensor.matmul_mx(
@@ -155,7 +159,7 @@ def tile_list_sum_largerpicks_othertable_levelled_rowshares_kernel(
         G = HALF // BUNDLE
         means = []
         for h in halves:
-            sums = sb.tile([P, G, PACK], F32, name=f"sums{h}", tag=("ws_raw", "sums1")[h], align_bytes=64)
+            sums = sb.tile([P, G, PACK], F32, name=f"sums{h}")
             nc.vector.tensor_reduce(
                 out=sums[:], in_=acc[h][:].rearrange("p t (g e) -> p g t e", e=BUNDLE), axis=AX.X, op=ALU.add
             )

@@ -40,11 +40,13 @@ def tile_list_sum_largerpicks_othertable_levelled_rowshares_kernel(
         list1 = sb.tile([P, J // 16], U16, name="list1")
         list2 = sb.tile([P, J // 16], U16, name="list2")
         list3 = sb.tile([P, J // 16], U16, name="list3")
-        x_pairs = [sb.tile([P, 2, T], F32, name=f"x{u}") for u in range(2)]
-        x_planes = [x_pairs[t // 2][:, t % 2, :] for t in range(PACK)]
+        x0 = sb.tile([P, T], F32, name="x0")
+        x1 = sb.tile([P, T], F32, name="x1")
+        x23 = sb.tile([P, 2, T], F32, name="x23")
+        x_planes = (x0[:], x1[:], x23[:, 0, :], x23[:, 1, :])
         fk_sb = sb.tile([P, PACK], F32, name="fk_sb")
         w_raw = sb.tile([P, R], U16, name="w_raw")
-        w2_raw = sb.tile([P, R], U32, name="w2_raw")
+        w2_raw = sb.tile([P, R], U32, name="w2_raw", tag="w2_raw")
         ws_raw = sb.tile([P, R], U8, name="ws_raw", tag="ws_raw", align_bytes=64)
         w2s_raw = sb.tile([P, R], U8, name="w2s_raw")
         xo_tab = sb.tile([P, Z], U32, name="xo_tab", tag="xo_tab", align_bytes=64)
@@ -58,23 +60,24 @@ def tile_list_sum_largerpicks_othertable_levelled_rowshares_kernel(
             nc.vector.memset(plane[:].bitcast(I32), 0)
 
         xv = xf.rearrange("(p t) c -> p t c", t=PACK)
+        nc.sync.dma_start(out=x0[:], in_=xv[:, 0, :])
         nc.sync.dma_start(list1[:], offs)
         nc.sync.dma_start(list2[:], offs2)
-        nc.sync.dma_start(list3[:], offs3)
         load_scale_rows(nc.scalar, w2s_raw, w2_scales, range(3))
         warm = sb.tile([P, 1], F32, name="warm")
         nc.vector.memset(warm[:], 0.0)
         nc.scalar.activation(warm[:], warm[:], ACT.Exp)
-        nc.sync.dma_start(out=x_pairs[0][:], in_=xv[:, 0:2, :])
-        nc.sync.dma_start(out=x_pairs[1][:], in_=xv[:, 2:4, :])
+        nc.sync.dma_start(out=x1[:], in_=xv[:, 1, :])
+        nc.sync.dma_start(out=x23[:], in_=xv[:, 2:4, :])
         nc.gpsimd.dma_start(out=fk_sb[:], in_=fk.rearrange("(p t) o -> p (t o)", t=PACK))
         load_scale_rows(nc.gpsimd, ws_raw, w_scales, range(3, 4))
-        load_scale_rows(nc.sync, w2s_raw, w2_scales, range(3, 4))
-        load_scale_rows(nc.sync, xos_tab, xo_scales, range(1))
         nc.sync.dma_start(out=xo_tab[:].bitcast(I32), in_=xo_words[0].rearrange("p n t -> p (n t)").bitcast(I32))
+        nc.sync.dma_start(list3[:], offs3)
+        load_scale_rows(nc.sync, w2s_raw, w2_scales, range(3, 4))
+        load_scale_rows(nc.sync, xos_tab, xo_scales, range(3))
         nc.sync.dma_start(out=w2_raw[:].bitcast(I32), in_=w2_words[0].rearrange("p n t -> p (n t)").bitcast(I32))
+        load_scale_rows(nc.sync, xos_tab, xo_scales, range(3, 4))
         nc.sync.dma_start(out=w_raw[:].bitcast(I32), in_=w_words[0].bitcast(I32))
-        load_scale_rows(nc.sync, xos_tab, xo_scales, range(1, 4))
         load_scale_rows(nc.sync, ws_raw, w_scales, range(3))
         nc.sync.dma_start(out=wb_sb[:].bitcast(I32), in_=wb_words[0].rearrange("p n t -> p (n t)").bitcast(I32))
         load_scale_rows(nc.sync, wbs_sb, wb_scales, range(4))
@@ -105,7 +108,7 @@ def tile_list_sum_largerpicks_othertable_levelled_rowshares_kernel(
         nc.vector.tensor_tensor(larger23[:], pick1[:, 2:4, :], pick2[:, 2:4, :], ALU.max)
         nc.vector.tensor_copy(xos_g[:], xos_tab[:].indirect(list3[:]))
         deal(nc.scalar.copy, w2_st, w2_raw, "p q t")
-        u_planes = sb.tile([P, PACK, J], BF16, name="u_planes")
+        u_planes = sb.tile([P, PACK, J], BF16, name="u_planes", tag="w2_raw")
         for t in range(2):
             nc.scalar.activation(u_planes[:, t, :], larger01[:, t, :], ACT.Copy, scale=fk_sb[:, t : t + 1])
         for j0 in range(0, J, HALF):

@@ -22,11 +22,21 @@ P = 128
 PACK = 4
 HALF = 128
 BUNDLE = 8
+QUADRANTS = 4
+LIST_ROWS = 16
+RUN = 4
+SCALAR_LIST2_PLANE = 2
 
 
-def load_scale_rows(queue, plane, scales, quadrants):
+def load_scale_rows(queue, scale_tile, scales, quadrants):
     for q in quadrants:
-        queue.dma_start(out=plane[32 * q : 32 * q + 4, :].bitcast(I32), in_=scales[0, 4 * q : 4 * q + 4, :].bitcast(I32))
+        queue.dma_start(
+            out=scale_tile[32 * q : 32 * q + 4, :].bitcast(I32), in_=scales[0, 4 * q : 4 * q + 4, :].bitcast(I32)
+        )
+
+
+def deal_columns(copy, dealt, raw, walk):
+    copy(dealt[:].rearrange("p (t q) -> " + walk, t=PACK), raw[:].rearrange("p (q t) -> " + walk, t=PACK))
 
 
 def tile_list_sum_largerpicks_othertable_levelled_rowshares_kernel(
@@ -37,9 +47,9 @@ def tile_list_sum_largerpicks_othertable_levelled_rowshares_kernel(
         sb = ctx.enter_context(tc.tile_pool(name="sb", bufs=1))
         ps = ctx.enter_context(tc.psum_pool(name="ps", bufs=1))
 
-        list1 = sb.tile([P, J // 16], U16, name="list1")
-        list2 = sb.tile([P, J // 16], U16, name="list2")
-        list3 = sb.tile([P, J // 16], U16, name="list3")
+        list1 = sb.tile([P, J // LIST_ROWS], U16, name="list1")
+        list2 = sb.tile([P, J // LIST_ROWS], U16, name="list2")
+        list3 = sb.tile([P, J // LIST_ROWS], U16, name="list3")
         x0 = sb.tile([P, T], F32, name="x0")
         x1 = sb.tile([P, T], F32, name="x1")
         x23 = sb.tile([P, 2, T], F32, name="x23")
@@ -56,58 +66,58 @@ def tile_list_sum_largerpicks_othertable_levelled_rowshares_kernel(
         bi_sb = sb.tile([P, N], F32, name="bi_sb")
 
         nc.gpsimd.memset(w2s_raw[:].bitcast(I32), 0)
-        for plane in (xos_tab, ws_raw, wbs_sb):
-            nc.vector.memset(plane[:].bitcast(I32), 0)
+        for scale_tile in (xos_tab, ws_raw, wbs_sb):
+            nc.vector.memset(scale_tile[:].bitcast(I32), 0)
 
+        all_but_last, last = range(QUADRANTS - 1), range(QUADRANTS - 1, QUADRANTS)
         xv = xf.rearrange("(p t) c -> p t c", t=PACK)
         nc.sync.dma_start(out=x0[:], in_=xv[:, 0, :])
         nc.sync.dma_start(list1[:], offs)
         nc.sync.dma_start(list2[:], offs2)
-        load_scale_rows(nc.scalar, w2s_raw, w2_scales, range(3))
+        load_scale_rows(nc.scalar, w2s_raw, w2_scales, all_but_last)
         warm = sb.tile([P, 1], F32, name="warm")
         nc.vector.memset(warm[:], 0.0)
         nc.scalar.activation(warm[:], warm[:], ACT.Exp)
         nc.sync.dma_start(out=x1[:], in_=xv[:, 1, :])
         nc.sync.dma_start(out=x23[:], in_=xv[:, 2:4, :])
         nc.gpsimd.dma_start(out=fk_sb[:], in_=fk.rearrange("(p t) o -> p (t o)", t=PACK))
-        load_scale_rows(nc.gpsimd, ws_raw, w_scales, range(3, 4))
+        load_scale_rows(nc.gpsimd, xos_tab, xo_scales, last)
+        load_scale_rows(nc.gpsimd, ws_raw, w_scales, last)
         nc.sync.dma_start(out=xo_tab[:].bitcast(I32), in_=xo_words[0].rearrange("p n t -> p (n t)").bitcast(I32))
         nc.sync.dma_start(list3[:], offs3)
-        load_scale_rows(nc.sync, w2s_raw, w2_scales, range(3, 4))
-        load_scale_rows(nc.sync, xos_tab, xo_scales, range(3))
+        load_scale_rows(nc.sync, w2s_raw, w2_scales, last)
+        load_scale_rows(nc.sync, xos_tab, xo_scales, all_but_last)
         nc.sync.dma_start(out=w2_raw[:].bitcast(I32), in_=w2_words[0].rearrange("p n t -> p (n t)").bitcast(I32))
-        load_scale_rows(nc.sync, xos_tab, xo_scales, range(3, 4))
         nc.sync.dma_start(out=w_raw[:].bitcast(I32), in_=w_words[0].bitcast(I32))
-        load_scale_rows(nc.sync, ws_raw, w_scales, range(3))
+        load_scale_rows(nc.sync, ws_raw, w_scales, all_but_last)
         nc.sync.dma_start(out=wb_sb[:].bitcast(I32), in_=wb_words[0].rearrange("p n t -> p (n t)").bitcast(I32))
-        load_scale_rows(nc.sync, wbs_sb, wb_scales, range(4))
+        load_scale_rows(nc.sync, wbs_sb, wb_scales, range(QUADRANTS))
         nc.sync.dma_start(out=bi_sb[:], in_=bi[0].partition_broadcast(P))
 
         w2_st = sb.tile([P, R], U32, name="w2_st", align_bytes=64)
         ws_st = sb.tile([P, R], U8, name="ws_st", align_bytes=64)
         w2s_st = sb.tile([P, R], U8, name="w2s_st", align_bytes=64)
+        deal_columns(nc.vector.tensor_copy, w2s_st, w2s_raw, "p t q")
 
-        def deal(copy, dst, raw, order):
-            copy(dst[:].rearrange("p (t q) -> " + order, t=PACK), raw[:].rearrange("p (q t) -> " + order, t=PACK))
-
-        deal(nc.vector.tensor_copy, w2s_st, w2s_raw, "p t q")
         pick1 = sb.tile([P, PACK, J], F32, name="pick1")
         pick2 = sb.tile([P, PACK, J], F32, name="pick2")
         xo_g = sb.tile([P, J], U32, name="xo_g", align_bytes=64)
         xos_g = sb.tile([P, J], U8, name="xos_g", align_bytes=64)
         for t in range(PACK):
             nc.scalar.activation(pick1[:, t, :], x_planes[t].indirect(list1[:]), ACT.Copy)
-            if t in (2,):
+            if t == SCALAR_LIST2_PLANE:
                 nc.scalar.activation(pick2[:, t, :], x_planes[t].indirect(list2[:]), ACT.Copy)
             else:
                 nc.vector.tensor_copy(pick2[:, t, :], x_planes[t].indirect(list2[:]))
+
         larger01 = sb.tile([P, 2, J], F32, name="larger01")
         nc.vector.tensor_tensor(larger01[:], pick1[:, 0:2, :], pick2[:, 0:2, :], ALU.max)
         nc.vector.tensor_copy(xo_g[:], xo_tab[:].indirect(list3[:]))
         larger23 = sb.tile([P, 2, J], F32, name="larger23", tag="xo_tab", align_bytes=64)
         nc.vector.tensor_tensor(larger23[:], pick1[:, 2:4, :], pick2[:, 2:4, :], ALU.max)
         nc.vector.tensor_copy(xos_g[:], xos_tab[:].indirect(list3[:]))
-        deal(nc.scalar.copy, w2_st, w2_raw, "p q t")
+
+        deal_columns(nc.scalar.copy, w2_st, w2_raw, "p q t")
         u_planes = sb.tile([P, PACK, J], BF16, name="u_planes", tag="w2_raw")
         for t in range(2):
             nc.scalar.activation(u_planes[:, t, :], larger01[:, t, :], ACT.Copy, scale=fk_sb[:, t : t + 1])
@@ -117,8 +127,8 @@ def tile_list_sum_largerpicks_othertable_levelled_rowshares_kernel(
                     u_planes[:, t, j0 : j0 + HALF], larger23[:, t - 2, j0 : j0 + HALF], ACT.Copy, scale=fk_sb[:, t : t + 1]
                 )
         w_st = sb.tile([P, R], U16, name="w_st", tag="xo_tab", align_bytes=64)
-        deal(nc.scalar.copy, w_st, w_raw, "p q t")
-        deal(nc.vector.tensor_copy, ws_st, ws_raw, "p t q")
+        deal_columns(nc.scalar.copy, w_st, w_raw, "p q t")
+        deal_columns(nc.vector.tensor_copy, ws_st, ws_raw, "p t q")
         u_all = sb.tile([P, J, PACK], BF16, name="u_all", tag="ws_raw", align_bytes=64)
 
         halves = range(J // HALF)
@@ -141,8 +151,8 @@ def tile_list_sum_largerpicks_othertable_levelled_rowshares_kernel(
             cols = slice(h * HALF, (h + 1) * HALF)
             u_bf = u_all[:, cols, :]
             nc.vector.tensor_copy(
-                u_bf.rearrange("p (c i) t -> p c t i", i=4),
-                u_planes[:, :, cols].rearrange("p t (c i) -> p c t i", i=4),
+                u_bf.rearrange("p (c i) t -> p c t i", i=RUN),
+                u_planes[:, :, cols].rearrange("p t (c i) -> p c t i", i=RUN),
             )
             uq = sb.tile([P, HALF], U32, name=f"uq{h}", align_bytes=64)
             us = sb.tile([P, HALF], U8, name=f"us{h}", align_bytes=64)
@@ -159,29 +169,29 @@ def tile_list_sum_largerpicks_othertable_levelled_rowshares_kernel(
                     stop=(t == PACK - 1),
                 )
 
-        G = HALF // BUNDLE
+        bundles = HALF // BUNDLE
         means = []
         for h in halves:
-            sums = sb.tile([P, G, PACK], F32, name=f"sums{h}")
+            sums = sb.tile([P, bundles, PACK], F32, name=f"sums{h}")
             nc.vector.tensor_reduce(
                 out=sums[:], in_=acc[h][:].rearrange("p t (g e) -> p g t e", e=BUNDLE), axis=AX.X, op=ALU.add
             )
-            mean = sb.tile([P, G, PACK], F32, name=f"mean{h}")
+            mean = sb.tile([P, bundles, PACK], F32, name=f"mean{h}")
             nc.scalar.activation(mean[:], sums[:], ACT.Copy, scale=1.0 / BUNDLE)
             means.append(mean)
 
         hids = []
         for h in halves:
-            hid = sb.tile([P, G, BUNDLE, PACK], BF16, name=f"hid{h}", align_bytes=64)
+            hid = sb.tile([P, bundles, BUNDLE, PACK], BF16, name=f"hid{h}", align_bytes=64)
             nc.vector.tensor_tensor(
                 hid[:],
                 acc[h][:].rearrange("p t (g e) -> p g e t", e=BUNDLE),
-                means[h][:].unsqueeze(2).to_broadcast([P, G, BUNDLE, PACK]),
+                means[h][:].unsqueeze(2).to_broadcast([P, bundles, BUNDLE, PACK]),
                 ALU.subtract,
             )
             hids.append(hid)
 
-        logits = []
+        products = []
         for h in halves:
             hq = sb.tile([P, HALF], U32, name=f"hq{h}", align_bytes=64)
             hs = sb.tile([P, HALF], U8, name=f"hs{h}", align_bytes=64)
@@ -196,23 +206,23 @@ def tile_list_sum_largerpicks_othertable_levelled_rowshares_kernel(
                 start=True,
                 stop=True,
             )
-            logits.append(prod)
+            products.append(prod)
 
         exps = []
         for h in halves:
             z = sb.tile([P, N], F32, name=f"z{h}")
-            nc.vector.scalar_tensor_tensor(z[:], logits[h][:], 0.7, bi_sb[:], ALU.mult, ALU.add)
+            nc.vector.scalar_tensor_tensor(z[:], products[h][:], 0.7, bi_sb[:], ALU.mult, ALU.add)
             neg_max = sb.tile([P, 1], F32, name=f"neg_max{h}")
             nc.vector.tensor_reduce(out=neg_max[:], in_=z[:], axis=AX.X, op=ALU.max, negate=True)
-            e = sb.tile([P, N], F32, name=f"e{h}")
+            ea = sb.tile([P, N], F32, name=f"e{h}")
             total = sb.tile([P, 1], F32, name=f"total{h}")
-            nc.scalar.activation(e[:], z[:], ACT.Exp, bias=neg_max[:], scale=1.0, accum_out=total[:])
-            exps.append((e, total))
+            nc.scalar.activation(ea[:], z[:], ACT.Exp, bias=neg_max[:], scale=1.0, accum_out=total[:])
+            exps.append((ea, total))
 
         for h in halves:
-            e, total = exps[h]
+            ea, total = exps[h]
             inv = sb.tile([P, 1], F32, name=f"inv{h}")
             nc.vector.reciprocal(inv[:], total[:])
             y = sb.tile([P, N], F32, name=f"y{h}")
-            nc.vector.tensor_scalar(y[:], e[:], inv[:], 256.0, ALU.mult, ALU.mult)
+            nc.vector.tensor_scalar(y[:], ea[:], inv[:], 256.0, ALU.mult, ALU.mult)
             nc.sync.dma_start(out=out[h * HALF : (h + 1) * HALF, :], in_=y[:])

from contextlib import ExitStack

import concourse.mybir as mybir

K, T, J, R, F, Z, N = 512, 512, 256, 512, 512, 1024, 256
FLOPS = 2 * K * R * J + 2 * F * R * J + 2 * R * J * N

F32 = mybir.dt.float32
BF16 = mybir.dt.bfloat16
I32 = mybir.dt.int32
U32 = mybir.dt.uint32
U16 = mybir.dt.uint16
U8 = mybir.dt.uint8
E4M3 = mybir.dt.float8_e4m3fn_x4
E5M2 = mybir.dt.float8_e5m2_x4
E2M1 = mybir.dt.float4_e2m1fn_x4
ALU = mybir.AluOpType
ACT = mybir.ActivationFunctionType
AX = mybir.AxisListType

P = 128
PACK = 4
HALF = 128
BUNDLE = 8
QUADRANTS = 4
LIST_ROWS = 16
RUN = 4
SCALAR_LIST2_PLANE = 2


def load_scale_rows(queue, scale_tile, scales, quadrants):
    for q in quadrants:
        queue.dma_start(
            out=scale_tile[32 * q : 32 * q + 4, :].bitcast(I32), in_=scales[0, 4 * q : 4 * q + 4, :].bitcast(I32)
        )


def deal_columns(copy, dealt, raw, walk):
    copy(dealt[:].rearrange("p (t q) -> " + walk, t=PACK), raw[:].rearrange("p (q t) -> " + walk, t=PACK))


def tile_list_sum_largerpicks_othertable_levelled_rowshares_kernel(
    tc, xf, fk, w_words, w_scales, xo_words, xo_scales, w2_words, w2_scales, wb_words, wb_scales, bi, offs, offs2, offs3, out
):
    nc = tc.nc
    with ExitStack() as ctx:
        sb = ctx.enter_context(tc.tile_pool(name="sb", bufs=1))
        ps = ctx.enter_context(tc.psum_pool(name="ps", bufs=1))

        list1 = sb.tile([P, J // LIST_ROWS], U16, name="list1")
        list2 = sb.tile([P, J // LIST_ROWS], U16, name="list2")
        list3 = sb.tile([P, J // LIST_ROWS], U16, name="list3")
        x0 = sb.tile([P, T], F32, name="x0")
        x1 = sb.tile([P, T], F32, name="x1")
        x23 = sb.tile([P, 2, T], F32, name="x23")
        x_planes = (x0[:], x1[:], x23[:, 0, :], x23[:, 1, :])
        fk_sb = sb.tile([P, PACK], F32, name="fk_sb")
        w_raw = sb.tile([P, R], U16, name="w_raw")
        w2_raw = sb.tile([P, R], U32, name="w2_raw", tag="w2_raw")
        ws_raw = sb.tile([P, R], U8, name="ws_raw", tag="ws_raw", align_bytes=64)
        w2s_raw = sb.tile([P, R], U8, name="w2s_raw")
        xo_tab = sb.tile([P, Z], U32, name="xo_tab", tag="xo_tab", align_bytes=64)
        xos_tab = sb.tile([P, Z], U8, name="xos_tab")
        wb_sb = sb.tile([P, N], U32, name="wb_sb", align_bytes=64)
        wbs_sb = sb.tile([P, N], U8, name="wbs_sb", align_bytes=64)
        bi_sb = sb.tile([P, N], F32, name="bi_sb")

        nc.gpsimd.memset(w2s_raw[:].bitcast(I32), 0)
        for scale_tile in (xos_tab, ws_raw, wbs_sb):
            nc.vector.memset(scale_tile[:].bitcast(I32), 0)

        all_but_last, last = range(QUADRANTS - 1), range(QUADRANTS - 1, QUADRANTS)
        xv = xf.rearrange("(p t) c -> p t c", t=PACK)
        nc.sync.dma_start(out=x0[:], in_=xv[:, 0, :])
        nc.sync.dma_start(list1[:], offs)
        nc.sync.dma_start(list2[:], offs2)
        load_scale_rows(nc.scalar, w2s_raw, w2_scales, all_but_last)
        warm = sb.tile([P, 1], F32, name="warm")
        nc.vector.memset(warm[:], 0.0)
        nc.scalar.activation(warm[:], warm[:], ACT.Exp)
        nc.sync.dma_start(out=x1[:], in_=xv[:, 1, :])
        nc.sync.dma_start(out=x23[:], in_=xv[:, 2:4, :])
        nc.gpsimd.dma_start(out=fk_sb[:], in_=fk.rearrange("(p t) o -> p (t o)", t=PACK))
        load_scale_rows(nc.gpsimd, xos_tab, xo_scales, last)
        load_scale_rows(nc.gpsimd, ws_raw, w_scales, last)
        nc.sync.dma_start(out=xo_tab[:].bitcast(I32), in_=xo_words[0].rearrange("p n t -> p (n t)").bitcast(I32))
        nc.sync.dma_start(list3[:], offs3)
        load_scale_rows(nc.sync, w2s_raw, w2_scales, last)
        load_scale_rows(nc.sync, xos_tab, xo_scales, all_but_last)
        nc.sync.dma_start(out=w2_raw[:].bitcast(I32), in_=w2_words[0].rearrange("p n t -> p (n t)").bitcast(I32))
        nc.sync.dma_start(out=w_raw[:].bitcast(I32), in_=w_words[0].bitcast(I32))
        load_scale_rows(nc.sync, ws_raw, w_scales, all_but_last)
        nc.sync.dma_start(out=wb_sb[:].bitcast(I32), in_=wb_words[0].rearrange("p n t -> p (n t)").bitcast(I32))
        load_scale_rows(nc.sync, wbs_sb, wb_scales, range(QUADRANTS))
        nc.sync.dma_start(out=bi_sb[:], in_=bi[0].partition_broadcast(P))

        w2_st = sb.tile([P, R], U32, name="w2_st", align_bytes=64)
        ws_st = sb.tile([P, R], U8, name="ws_st", align_bytes=64)
        w2s_st = sb.tile([P, R], U8, name="w2s_st", align_bytes=64)
        deal_columns(nc.vector.tensor_copy, w2s_st, w2s_raw, "p t q")

        pick1 = sb.tile([P, PACK, J], F32, name="pick1")
        pick2 = sb.tile([P, PACK, J], F32, name="pick2")
        xo_g = sb.tile([P, J], U32, name="xo_g", align_bytes=64)
        xos_g = sb.tile([P, J], U8, name="xos_g", align_bytes=64)
        for t in range(PACK):
            nc.scalar.activation(pick1[:, t, :], x_planes[t].indirect(list1[:]), ACT.Copy)
            if t == SCALAR_LIST2_PLANE:
                nc.scalar.activation(pick2[:, t, :], x_planes[t].indirect(list2[:]), ACT.Copy)
            else:
                nc.vector.tensor_copy(pick2[:, t, :], x_planes[t].indirect(list2[:]))

        larger01 = sb.tile([P, 2, J], F32, name="larger01")
        nc.vector.tensor_tensor(larger01[:], pick1[:, 0:2, :], pick2[:, 0:2, :], ALU.max)
        nc.vector.tensor_copy(xo_g[:], xo_tab[:].indirect(list3[:]))
        larger23 = sb.tile([P, 2, J], F32, name="larger23", tag="xo_tab", align_bytes=64)
        nc.vector.tensor_tensor(larger23[:], pick1[:, 2:4, :], pick2[:, 2:4, :], ALU.max)
        nc.vector.tensor_copy(xos_g[:], xos_tab[:].indirect(list3[:]))

        deal_columns(nc.scalar.copy, w2_st, w2_raw, "p q t")
        u_planes = sb.tile([P, PACK, J], BF16, name="u_planes", tag="w2_raw")
        for t in range(2):
            nc.scalar.activation(u_planes[:, t, :], larger01[:, t, :], ACT.Copy, scale=fk_sb[:, t : t + 1])
        for j0 in range(0, J, HALF):
            for t in range(2, PACK):
                nc.scalar.activation(
                    u_planes[:, t, j0 : j0 + HALF], larger23[:, t - 2, j0 : j0 + HALF], ACT.Copy, scale=fk_sb[:, t : t + 1]
                )
        w_st = sb.tile([P, R], U16, name="w_st", tag="xo_tab", align_bytes=64)
        deal_columns(nc.scalar.copy, w_st, w_raw, "p q t")
        deal_columns(nc.vector.tensor_copy, ws_st, ws_raw, "p t q")
        u_all = sb.tile([P, J, PACK], BF16, name="u_all", tag="ws_raw", align_bytes=64)

        halves = range(J // HALF)
        acc = [ps.tile([P, PACK, HALF], F32, name=f"acc{h}") for h in halves]
        for h in halves:
            cols = slice(h * HALF, (h + 1) * HALF)
            for t in range(PACK):
                st = slice(t * P, (t + 1) * P)
                nc.tensor.matmul_mx(
                    out=acc[h][:, t, :],
                    lhsT=w2_st[:, st].bitcast(E5M2),
                    lhsT_scale=w2s_st[:, st],
                    rhs=xo_g[:, cols].bitcast(E4M3),
                    rhs_scale=xos_g[:, cols],
                    start=(t == 0),
                    stop=False,
                )

        for h in halves:
            cols = slice(h * HALF, (h + 1) * HALF)
            u_bf = u_all[:, cols, :]
            nc.vector.tensor_copy(
                u_bf.rearrange("p (c i) t -> p c t i", i=RUN),
                u_planes[:, :, cols].rearrange("p t (c i) -> p c t i", i=RUN),
            )
            uq = sb.tile([P, HALF], U32, name=f"uq{h}", align_bytes=64)
            us = sb.tile([P, HALF], U8, name=f"us{h}", align_bytes=64)
            nc.vector.quantize_mx(out=uq[:].bitcast(E4M3), scales=us[:], in_=u_bf.rearrange("p j t -> p (j t)"))
            for t in range(PACK):
                st = slice(t * P, (t + 1) * P)
                nc.tensor.matmul_mx(
                    out=acc[h][:, t, :],
                    lhsT=w_st[:, st].bitcast(E2M1),
                    lhsT_scale=ws_st[:, st],
                    rhs=uq[:].bitcast(E4M3),
                    rhs_scale=us[:],
                    start=False,
                    stop=(t == PACK - 1),
                )

        bundles = HALF // BUNDLE
        means = []
        for h in halves:
            sums = sb.tile([P, bundles, PACK], F32, name=f"sums{h}")
            nc.vector.tensor_reduce(
                out=sums[:], in_=acc[h][:].rearrange("p t (g e) -> p g t e", e=BUNDLE), axis=AX.X, op=ALU.add
            )
            mean = sb.tile([P, bundles, PACK], F32, name=f"mean{h}")
            nc.scalar.activation(mean[:], sums[:], ACT.Copy, scale=1.0 / BUNDLE)
            means.append(mean)

        hids = []
        for h in halves:
            hid = sb.tile([P, bundles, BUNDLE, PACK], BF16, name=f"hid{h}", align_bytes=64)
            nc.vector.tensor_tensor(
                hid[:],
                acc[h][:].rearrange("p t (g e) -> p g e t", e=BUNDLE),
                means[h][:].unsqueeze(2).to_broadcast([P, bundles, BUNDLE, PACK]),
                ALU.subtract,
            )
            hids.append(hid)

        products = []
        for h in halves:
            hq = sb.tile([P, HALF], U32, name=f"hq{h}", align_bytes=64)
            hs = sb.tile([P, HALF], U8, name=f"hs{h}", align_bytes=64)
            nc.vector.quantize_mx(out=hq[:].bitcast(E5M2), scales=hs[:], in_=hids[h][:].rearrange("p g e t -> p (g e t)"))
            prod = ps.tile([P, N], F32, name=f"prod{h}")
            nc.tensor.matmul_mx(
                out=prod[:],
                lhsT=hq[:].bitcast(E5M2),
                lhsT_scale=hs[:],
                rhs=wb_sb[:].bitcast(E5M2),
                rhs_scale=wbs_sb[:],
                start=True,
                stop=True,
            )
            products.append(prod)

        exps = []
        for h in halves:
            z = sb.tile([P, N], F32, name=f"z{h}")
            nc.vector.scalar_tensor_tensor(z[:], products[h][:], 0.7, bi_sb[:], ALU.mult, ALU.add)
            neg_max = sb.tile([P, 1], F32, name=f"neg_max{h}")
            nc.vector.tensor_reduce(out=neg_max[:], in_=z[:], axis=AX.X, op=ALU.max, negate=True)
            ea = sb.tile([P, N], F32, name=f"e{h}")
            total = sb.tile([P, 1], F32, name=f"total{h}")
            nc.scalar.activation(ea[:], z[:], ACT.Exp, bias=neg_max[:], scale=1.0, accum_out=total[:])
            exps.append((ea, total))

        for h in halves:
            ea, total = exps[h]
            inv = sb.tile([P, 1], F32, name=f"inv{h}")
            nc.vector.reciprocal(inv[:], total[:])
            y = sb.tile([P, N], F32, name=f"y{h}")
            nc.vector.tensor_scalar(y[:], ea[:], inv[:], 256.0, ALU.mult, ALU.mult)
            nc.sync.dma_start(out=out[h * HALF : (h + 1) * HALF, :], in_=y[:])
